import numpy as np, ml_dtypes
CORES = [3,5,43,45,51,53,67,69,75,77,83,85,91,93,115,117]
N = 16
TK = 128
COEF = [[3,1,1,1,1,1,1,1,1,1,1,1,1,1,1,1],[1,3,1,1,1,1,1,1,1,1,1,1,1,1,1,1],[1,1,3,1,1,1,1,1,1,1,1,1,1,1,1,1],[1,1,1,3,1,1,1,1,1,1,1,1,1,1,1,1],[1,1,1,1,3,1,1,1,1,1,1,1,1,1,1,1],[1,1,1,1,1,3,1,1,1,1,1,1,1,1,1,1],[1,1,1,1,1,1,3,1,1,1,1,1,1,1,1,1],[1,1,1,1,1,1,1,3,1,1,1,1,1,1,1,1],[1,1,1,1,1,1,1,1,3,1,1,1,1,1,1,1],[1,1,1,1,1,1,1,1,1,3,1,1,1,1,1,1],[1,1,1,1,1,1,1,1,1,1,3,1,1,1,1,1],[1,1,1,1,1,1,1,1,1,1,1,3,1,1,1,1],[1,1,1,1,1,1,1,1,1,1,1,1,3,1,1,1],[1,1,1,1,1,1,1,1,1,1,1,1,1,3,1,1],[1,1,1,1,1,1,1,1,1,1,1,1,1,1,3,1],[1,1,1,1,1,1,1,1,1,1,1,1,1,1,1,3]]
def setup_inputs(rng):
    return {"x": rng.standard_normal((N, 128, TK), dtype=np.float32).astype(ml_dtypes.bfloat16), "a": (rng.standard_normal((N, 128, 128), dtype=np.float32) / 11).astype(ml_dtypes.bfloat16)}
def setup_inputs_big(rng):
    d = setup_inputs(rng)
    for k in ("x", "a"): d[k] = (d[k].astype(np.float32) * 1024.0).astype(d[k].dtype)
    return d
def setup_inputs_small(rng):
    d = setup_inputs(rng)
    for k in ("x", "a"): d[k] = (d[k].astype(np.float32) * (1 / 1024.0)).astype(d[k].dtype)
    return d
def setup_inputs_apart(rng):
    d = setup_inputs(rng)
    f = (10.0 ** rng.permutation(np.linspace(-1.5, 1.5, N))).astype(np.float32).reshape(N, 1, 1)
    for k in ("x", "a"): d[k] = (d[k].astype(np.float32) * f).astype(d[k].dtype)
    return d
def reference(x, a):
    X, A = x.astype(np.float64), a.astype(np.float64)
    y = np.stack([A[r].T @ sum(COEF[r][j] * X[j] for j in range(N)) for r in range(N)])
    return {"y": y.astype(ml_dtypes.bfloat16)}

@@ -1,0 +1,195 @@
+import comms_topo
+from concourse.bass import DstId, RemoteDMATransfer
+
+CORES = [3, 5, 43, 45, 51, 53, 67, 69, 75, 77, 83, 85, 91, 93, 115, 117]
+P, W = 128, 128
+
+
+def _engines(mask):
+    return [e for e in range(mask.bit_length()) if (mask >> e) & 1]
+
+
+def _mask_of(engines):
+    m = 0
+    for e in engines:
+        m |= 1 << e
+    return m
+
+
+def _pow2_floor(n):
+    k = 1
+    while 2 * k <= n:
+        k *= 2
+    return k
+
+
+def _make_plan(cores, topo):
+    planes = []
+    for c in cores:
+        for pl in planes:
+            if topo.chip(pl[0]) == topo.chip(c) or topo.same_plane(topo.chip(pl[0]), topo.chip(c)):
+                pl.append(c)
+                break
+        else:
+            planes.append([c])
+    slices, jobs = [], []
+    for ci, mem in enumerate(planes):
+        far = [c for c in cores if c not in mem]
+        ported = [m for m in mem if all(topo.may_write(m, d) for d in far)]
+        inner = [m for m in mem if m not in ported]
+        k = _pow2_floor(min(len(ported), len(inner)))
+        slices.append(k)
+        room = len(_engines(topo.mask(mem[0], far[0])))
+        spare = ported[k:k + (room - 2 * k) // k]
+        load = {}
+        for m in ported[:k]:
+            load[topo.chip(m)] = load.get(topo.chip(m), 0) + 1
+        for m in spare:
+            load[topo.chip(m)] = load.get(topo.chip(m), 0) + k
+        own_in = []
+        for s in range(k):
+            b = min([m for m in inner if m not in own_in], key=lambda m: load.get(topo.chip(m), 0))
+            load[topo.chip(b)] = load.get(topo.chip(b), 0) + 1
+            own_in.append(b)
+        t = 0
+        if spare:
+            t = min(range(len(far) // len(spare) + 1),
+                    key=lambda q: max(len(far) - q * len(spare), k * (q + 1)))
+        taken = {}
+        left = list(far)
+        for m in spare:
+            pick = sorted(left, key=lambda d: not topo.mates(topo.chip(m), topo.chip(d)))[:t]
+            taken[m] = pick
+            left = [d for d in left if d not in pick]
+        for s in range(k):
+            jobs.append([ci, own_in[s], s, [m for m in mem if m != own_in[s]]])
+            if spare:
+                jobs.append([ci, ported[s], s, list(left)])
+                for i, m in enumerate(spare):
+                    jobs.append([ci, m, s, taken[m] + ([own_in[s]] if i == 0 else [])])
+            else:
+                jobs.append([ci, ported[s], s, list(left) + [own_in[s]]])
+    send = {}
+    for ci, mem in enumerate(planes):
+        for m in mem:
+            todo = [(o, s) for (cj, o, s, _) in jobs if cj == ci and o != m]
+            todo.sort(key=lambda os: topo.chip(os[0]) == topo.chip(m))
+            used, out = [], []
+            for (o, s) in todo:
+                e = [e for e in _engines(topo.mask(m, o)) if e not in used][0]
+                used.append(e)
+                out.append((o, s, [e]))
+            send[m] = out
+    serve = {}
+    for c in cores:
+        mine = [j for j in jobs if j[1] == c]
+        if not mine:
+            continue
+        common = None
+        for (_, _, _, dests) in mine:
+            for d in dests:
+                common = topo.mask(c, d) if common is None else common & topo.mask(c, d)
+        eng = _engines(common)
+        per = _pow2_floor(len(eng) // len(mine))
+        serve[c] = [(ci, s, dests, eng[i * per:(i + 1) * per]) for i, (ci, _, s, dests) in enumerate(mine)]
+    got = {c: 0 for c in cores}
+    for m in send:
+        for (o, s, e) in send[m]:
+            got[o] += len(e)
+    arrive = {c: [0] * len(planes) for c in cores}
+    cover = {c: [] for c in cores}
+    for c in serve:
+        for (ci, s, dests, e) in serve[c]:
+            for d in dests:
+                assert d != c and topo.may_write(c, d)
+                arrive[d][ci] += len(e)
+                cover[d].append((ci, s))
+    want = sorted((ci, s) for ci in range(len(planes)) for s in range(slices[ci]))
+    for c in cores:
+        assert sorted(cover[c]) == want
+    return {"planes": planes, "slices": slices, "send": send, "serve": serve, "got": got, "arrive": arrive}
+
+
+PLAN = _make_plan(CORES, comms_topo)
+
+SCRATCH = {
+    "a_sb": ("sbuf", [P, W], "bfloat16"),
+    "x_sb": ("sbuf", [P, W], "bfloat16"),
+    "y_sb": ("sbuf", [P, W], "bfloat16"),
+    "acc": ("psum", [P, W], "float32"),
+}
+SEMAPHORES = ["xd", "ld", "got", "sent", "mm", "cp", "st"]
+for _ci, _k in enumerate(PLAN["slices"]):
+    _n = len(PLAN["planes"][_ci])
+    SCRATCH["xd%d" % _ci] = ("dram", [_k, P, W // _k], "bfloat16")
+    SCRATCH["land%d" % _ci] = ("dram", [_k * _n, P, W // _k], "bfloat16")
+    SCRATCH["sum%d" % _ci] = ("dram", [_k, P, W // _k], "bfloat16")
+    SCRATCH["s%d_sb" % _ci] = ("sbuf", [P, W], "bfloat16")
+    SEMAPHORES += ["sum%d" % _ci, "in%d" % _ci]
+
+
+def rank_program(g, core, T, topo):
+    rank = T.rank_of(core)
+    if rank is None:
+        return
+    assert list(T.cores) == CORES
+    coef = T.tables["COEF"]
+    u = coef[0][1]
+    assert all(coef[r][j] == u for r in range(len(CORES)) for j in range(len(CORES)) if r != j) and u >= 1
+    extra = coef[rank][rank] - u
+    assert extra >= 0
+
+    planes = PLAN["planes"]
+    mine = [ci for ci, mem in enumerate(planes) if core in mem][0]
+    mem = planes[mine]
+    xd, land = T["xd%d" % mine], T["land%d" % mine]
+
+    def dst_id(c):
+        rid, pid, _ = topo.addr(c)
+        return DstId(rid=rid, pnc=pid)
+
+    g.sync.dma_start(xd[:], T.x[:]).then_inc(T.sem.xd, 16)
+    g.sync.dma_start(T.a_sb[:], T.a[:]).then_inc(T.sem.ld, 16)
+    g.sync.dma_start(T.x_sb[:], T.x[:]).then_inc(T.sem.ld, 16)
+
+    sent = 0
+    g.wait_ge(T.sem.xd, 16)
+    out = []
+    for (o, s, eng) in PLAN["send"][core]:
+        out.append(RemoteDMATransfer(dst_ids=[dst_id(o)], dma_engine_mask=_mask_of(eng), remote_sem=T.sem.got,
+                                     src=xd[s], dst=land[s * len(mem) + mem.index(core)], alu_op=0))
+        sent += len(eng)
+    g.remote_dma_fused(out, local_sem=T.sem.sent)
+
+    if core in PLAN["serve"]:
+        g.wait_ge(T.sem.got, PLAN["got"][core])
+        out = []
+        for (ci, s, dests, eng) in PLAN["serve"][core]:
+            srcs = [xd[s] if m == core else land[s * len(mem) + i] for i, m in enumerate(mem)]
+            out.append(RemoteDMATransfer(dst_ids=[dst_id(d) for d in dests], dma_engine_mask=_mask_of(eng),
+                                         remote_sem=T.sem["sum%d" % ci], srcs=srcs,
+                                         dsts=[T["sum%d" % ci][s] for _ in dests], alu_op=1))
+            sent += len(eng)
+        g.remote_dma_fused(out, local_sem=T.sem.sent)
+    g.wait_ge(T.sem.sent, sent)
+
+    order = [mine] + [ci for ci in range(len(planes)) if ci != mine]
+    for i, ci in enumerate(order):
+        q = g.sync if i % 2 == 0 else g.scalar
+        q.wait_ge(T.sem["sum%d" % ci], PLAN["arrive"][core][ci])
+        q.dma_start(T["s%d_sb" % ci][:], T["sum%d" % ci][:]).then_inc(T.sem["in%d" % ci], 16)
+
+    ops = [(T.x_sb, None)] * extra
+    for ci in order:
+        ops += [(T["s%d_sb" % ci], T.sem["in%d" % ci])] + [(T["s%d_sb" % ci], None)] * (u - 1)
+    g.tensor.wait_ge(T.sem.ld, 32)
+    for i, (rhs, sem) in enumerate(ops):
+        if sem is not None:
+            g.tensor.wait_ge(sem, 16)
+        mm = g.tensor.matmul(T.acc[:], T.a_sb[:], rhs[:], i == 0, i == len(ops) - 1)
+    mm.then_inc(T.sem.mm, 1)
+    g.vector.wait_ge(T.sem.mm, 1)
+    g.vector.tensor_copy(T.y_sb[:], T.acc[:]).then_inc(T.sem.cp, 1)
+    g.sync.wait_ge(T.sem.cp, 1)
+    g.sync.dma_start(T.y[:], T.y_sb[:]).then_inc(T.sem.st, 16)
+    g.sync.wait_ge(T.sem.st, 16)

@@ -23,6 +23,11 @@ def _pow2_floor(n):
     return k
 
 
+def _turn(lst, s, k):
+    o = (s * len(lst)) // k
+    return lst[o:] + lst[:o]
+
+
 def _make_plan(cores, topo):
     planes = []
     for c in cores:
@@ -32,100 +37,122 @@ def _make_plan(cores, topo):
                 break
         else:
             planes.append([c])
-    slices, jobs = [], []
-    for ci, mem in enumerate(planes):
+    npl = len(planes)
+
+    def cut(k):
+        w = -(-P // k)
+        w += (-w) % npl
+        return [w] * (k - 1) + [P - w * (k - 1)]
+
+    who = []
+    for mem in planes:
         far = [c for c in cores if c not in mem]
         ported = [m for m in mem if all(topo.may_write(m, d) for d in far)]
-        inner = [m for m in mem if m not in ported]
-        k = _pow2_floor(min(len(ported), len(inner)))
-        slices.append(k)
-        room = len(_engines(topo.mask(mem[0], far[0])))
-        spare = ported[k:k + (room - 2 * k) // k]
+        who.append((far, ported, [m for m in mem if m not in ported]))
+
+    def work(ci, k):
+        return (len(planes[ci]) + max(len(who[ci][0]) + 1, len(cores) // 2)) * cut(k)[0]
+
+    kmax = [min(len(p), len(i)) for (_, p, i) in who]
+    bound = max(min(work(ci, kmax[ci]), work(ci, _pow2_floor(kmax[ci]))) for ci in range(npl))
+    widths, jobs = [], []
+    for ci, mem in enumerate(planes):
+        far, ported, inner = who[ci]
+        k = _pow2_floor(kmax[ci]) if work(ci, _pow2_floor(kmax[ci])) <= bound else kmax[ci]
+        widths.append(cut(k))
         load = {}
         for m in ported[:k]:
             load[topo.chip(m)] = load.get(topo.chip(m), 0) + 1
-        for m in spare:
-            load[topo.chip(m)] = load.get(topo.chip(m), 0) + k
         own_in = []
         for s in range(k):
             b = min([m for m in inner if m not in own_in], key=lambda m: load.get(topo.chip(m), 0))
             load[topo.chip(b)] = load.get(topo.chip(b), 0) + 1
             own_in.append(b)
-        t = 0
-        if spare:
-            t = min(range(len(far) // len(spare) + 1),
-                    key=lambda q: max(len(far) - q * len(spare), k * (q + 1)))
-        taken = {}
-        left = list(far)
-        for m in spare:
-            pick = sorted(left, key=lambda d: not topo.mates(topo.chip(m), topo.chip(d)))[:t]
-            taken[m] = pick
-            left = [d for d in left if d not in pick]
         for s in range(k):
-            jobs.append([ci, own_in[s], s, [m for m in mem if m != own_in[s]]])
-            if spare:
-                jobs.append([ci, ported[s], s, list(left)])
-                for i, m in enumerate(spare):
-                    jobs.append([ci, m, s, taken[m] + ([own_in[s]] if i == 0 else [])])
-            else:
-                jobs.append([ci, ported[s], s, list(left) + [own_in[s]]])
+            p, b = ported[s], own_in[s]
+            free = sorted([m for m in mem if m not in (p, b)], key=lambda m: topo.chip(m) != topo.chip(p))
+            take = free[:max(0, (len(free) - len(far)) // 2)]
+            jobs.append([ci, b, s, _turn([m for m in mem if m != b and m not in take], s, k)])
+            jobs.append([ci, p, s, _turn(list(far), s, k) + take + [b]])
+    groups, place = [], []
+    for ci in range(npl):
+        gr, pl, row = [], [], 0
+        for w in widths[ci]:
+            if not gr or gr[-1][1] != w:
+                gr.append([row, w, 0])
+            pl.append((len(gr) - 1, gr[-1][2]))
+            gr[-1][2] += 1
+            row += w
+        groups.append(gr)
+        place.append(pl)
     send = {}
     for ci, mem in enumerate(planes):
         for m in mem:
-            todo = [(o, s) for (cj, o, s, _) in jobs if cj == ci and o != m]
-            todo.sort(key=lambda os: topo.chip(os[0]) == topo.chip(m))
-            used, out = [], []
-            for (o, s) in todo:
-                e = [e for e in _engines(topo.mask(m, o)) if e not in used][0]
-                used.append(e)
-                out.append((o, s, [e]))
-            send[m] = out
+            eng = _engines(topo.mask(m, who[ci][0][0]))
+            calls = []
+            for gi in range(len(groups[ci])):
+                trs = []
+                for s in range(len(widths[ci])):
+                    if place[ci][s][0] != gi:
+                        continue
+                    ds = [o for (cj, o, s2, _) in jobs if cj == ci and s2 == s and o != m]
+                    ds.sort(key=lambda o: topo.chip(o) == topo.chip(m))
+                    assert all(topo.mask(m, o) & _mask_of(eng) == _mask_of(eng) for o in ds)
+                    trs.append((ds, s))
+                per = _pow2_floor(len(eng) // len(trs))
+                calls.append([(ds, s, eng[i * per:(i + 1) * per]) for i, (ds, s) in enumerate(trs)])
+            send[m] = calls
     serve = {}
-    for c in cores:
-        mine = [j for j in jobs if j[1] == c]
-        if not mine:
-            continue
+    for (ci, c, s, dests) in jobs:
+        assert c not in serve
         common = None
-        for (_, _, _, dests) in mine:
-            for d in dests:
-                common = topo.mask(c, d) if common is None else common & topo.mask(c, d)
-        eng = _engines(common)
-        per = _pow2_floor(len(eng) // len(mine))
-        serve[c] = [(ci, s, dests, eng[i * per:(i + 1) * per]) for i, (ci, _, s, dests) in enumerate(mine)]
+        for d in dests:
+            common = topo.mask(c, d) if common is None else common & topo.mask(c, d)
+        serve[c] = (ci, s, dests, _engines(common))
     got = {c: 0 for c in cores}
     for m in send:
-        for (o, s, e) in send[m]:
-            got[o] += len(e)
-    arrive = {c: [0] * len(planes) for c in cores}
+        for call in send[m]:
+            for (ds, s, e) in call:
+                for o in ds:
+                    got[o] += len(e)
+    arrive = {c: {} for c in cores}
     cover = {c: [] for c in cores}
     for c in serve:
-        for (ci, s, dests, e) in serve[c]:
-            for d in dests:
-                assert d != c and topo.may_write(c, d)
-                arrive[d][ci] += len(e)
-                cover[d].append((ci, s))
-    want = sorted((ci, s) for ci in range(len(planes)) for s in range(slices[ci]))
+        ci, s, dests, e = serve[c]
+        for d in dests:
+            assert d != c and topo.may_write(c, d)
+            key = (ci, place[ci][s][0])
+            arrive[d][key] = arrive[d].get(key, 0) + len(e)
+            cover[d].append((ci, s))
+    want = sorted((ci, s) for ci in range(npl) for s in range(len(widths[ci])))
     for c in cores:
         assert sorted(cover[c]) == want
-    return {"planes": planes, "slices": slices, "send": send, "serve": serve, "got": got, "arrive": arrive}
+    return {"planes": planes, "groups": groups, "place": place, "send": send, "serve": serve, "got": got,
+            "arrive": arrive}
 
 
 PLAN = _make_plan(CORES, comms_topo)
+NPL = len(PLAN["planes"])
+H = P // NPL
+assert H * NPL == P and H % 32 == 0
 
 SCRATCH = {
-    "a_sb": ("sbuf", [P, W], "bfloat16"),
-    "x_sb": ("sbuf", [P, W], "bfloat16"),
+    "a_sb": ("sbuf", [P, NPL * W], "bfloat16"),
+    "x_sb": ("sbuf", [H, NPL * W], "bfloat16"),
+    "s_sb": ("sbuf", [P, NPL * W], "bfloat16"),
     "y_sb": ("sbuf", [P, W], "bfloat16"),
     "acc": ("psum", [P, W], "float32"),
 }
-SEMAPHORES = ["xd", "ld", "got", "sent", "mm", "cp", "st"]
-for _ci, _k in enumerate(PLAN["slices"]):
+SEMAPHORES = ["ld", "got", "sent", "mm", "cp", "st"]
+for _ci, _gr in enumerate(PLAN["groups"]):
     _n = len(PLAN["planes"][_ci])
-    SCRATCH["xd%d" % _ci] = ("dram", [_k, P, W // _k], "bfloat16")
-    SCRATCH["land%d" % _ci] = ("dram", [_k * _n, P, W // _k], "bfloat16")
-    SCRATCH["sum%d" % _ci] = ("dram", [_k, P, W // _k], "bfloat16")
-    SCRATCH["s%d_sb" % _ci] = ("sbuf", [P, W], "bfloat16")
-    SEMAPHORES += ["sum%d" % _ci, "in%d" % _ci]
+    for _gi, (_row, _w, _cnt) in enumerate(_gr):
+        SCRATCH["xd%d_%d" % (_ci, _gi)] = ("dram", [_cnt, P, _w], "bfloat16")
+        SCRATCH["land%d_%d" % (_ci, _gi)] = ("dram", [_n, P, _w], "bfloat16")
+        SCRATCH["sum%d_%d" % (_ci, _gi)] = ("dram", [_cnt, P, _w], "bfloat16")
+        SEMAPHORES += ["sum%d_%d" % (_ci, _gi), "in%d_%d" % (_ci, _gi)]
+for _gi in range(max(len(_gr) for _gr in PLAN["groups"])):
+    SEMAPHORES.append("xd%d" % _gi)
 
 
 def rank_program(g, core, T, topo):
@@ -139,54 +166,69 @@ def rank_program(g, core, T, topo):
     extra = coef[rank][rank] - u
     assert extra >= 0
 
-    planes = PLAN["planes"]
+    planes, groups, place = PLAN["planes"], PLAN["groups"], PLAN["place"]
     mine = [ci for ci, mem in enumerate(planes) if core in mem][0]
     mem = planes[mine]
-    xd, land = T["xd%d" % mine], T["land%d" % mine]
+    queues = [g.sync, g.scalar]
 
     def dst_id(c):
         rid, pid, _ = topo.addr(c)
         return DstId(rid=rid, pnc=pid)
 
-    g.sync.dma_start(xd[:], T.x[:]).then_inc(T.sem.xd, 16)
-    g.sync.dma_start(T.a_sb[:], T.a[:]).then_inc(T.sem.ld, 16)
+    def xd(s):
+        gi, i = place[mine][s]
+        return T["xd%d_%d" % (mine, gi)][i]
+
+    for gi, (row, w, cnt) in enumerate(groups[mine]):
+        queues[gi % 2].dma_start(T["xd%d_%d" % (mine, gi)][:], T.x[row:row + w * cnt, :]).then_inc(T.sem["xd%d" % gi], 16)
+    for ci in range(NPL):
+        g.sync.dma_start(T.a_sb[ci * H:(ci + 1) * H, :], T.a[:]).then_inc(T.sem.ld, 16)
     g.sync.dma_start(T.x_sb[:], T.x[:]).then_inc(T.sem.ld, 16)
 
     sent = 0
-    g.wait_ge(T.sem.xd, 16)
-    out = []
-    for (o, s, eng) in PLAN["send"][core]:
-        out.append(RemoteDMATransfer(dst_ids=[dst_id(o)], dma_engine_mask=_mask_of(eng), remote_sem=T.sem.got,
-                                     src=xd[s], dst=land[s * len(mem) + mem.index(core)], alu_op=0))
-        sent += len(eng)
-    g.remote_dma_fused(out, local_sem=T.sem.sent)
-
-    if core in PLAN["serve"]:
-        g.wait_ge(T.sem.got, PLAN["got"][core])
+    for gi, call in enumerate(PLAN["send"][core]):
+        g.wait_ge(T.sem["xd%d" % gi], 16)
         out = []
-        for (ci, s, dests, eng) in PLAN["serve"][core]:
-            srcs = [xd[s] if m == core else land[s * len(mem) + i] for i, m in enumerate(mem)]
-            out.append(RemoteDMATransfer(dst_ids=[dst_id(d) for d in dests], dma_engine_mask=_mask_of(eng),
-                                         remote_sem=T.sem["sum%d" % ci], srcs=srcs,
-                                         dsts=[T["sum%d" % ci][s] for _ in dests], alu_op=1))
+        for (ds, s, eng) in call:
+            out.append(RemoteDMATransfer(dst_ids=[dst_id(o) for o in ds], dma_engine_mask=_mask_of(eng),
+                                         remote_sem=T.sem.got, srcs=[xd(s)],
+                                         dsts=[T["land%d_%d" % (mine, gi)][mem.index(core)] for _ in ds], alu_op=0))
             sent += len(eng)
         g.remote_dma_fused(out, local_sem=T.sem.sent)
+
+    if core in PLAN["serve"]:
+        ci, s, dests, eng = PLAN["serve"][core]
+        gi, i = place[ci][s]
+        g.wait_ge(T.sem.got, PLAN["got"][core])
+        srcs = [xd(s) if m == core else T["land%d_%d" % (ci, gi)][j] for j, m in enumerate(mem)]
+        g.remote_dma_fused([RemoteDMATransfer(dst_ids=[dst_id(d) for d in dests], dma_engine_mask=_mask_of(eng),
+                                              remote_sem=T.sem["sum%d_%d" % (ci, gi)], srcs=srcs,
+                                              dsts=[T["sum%d_%d" % (ci, gi)][i] for _ in dests], alu_op=1)],
+                           local_sem=T.sem.sent)
+        sent += len(eng)
     g.wait_ge(T.sem.sent, sent)
 
-    order = [mine] + [ci for ci in range(len(planes)) if ci != mine]
-    for i, ci in enumerate(order):
-        q = g.sync if i % 2 == 0 else g.scalar
-        q.wait_ge(T.sem["sum%d" % ci], PLAN["arrive"][core][ci])
-        q.dma_start(T["s%d_sb" % ci][:], T["sum%d" % ci][:]).then_inc(T.sem["in%d" % ci], 16)
+    loads = sorted((gi, ci) for ci in range(NPL) for gi in range(len(groups[ci])))
+    for i, (gi, ci) in enumerate(loads):
+        row, w, cnt = groups[ci][gi]
+        q = queues[i % 2]
+        q.wait_ge(T.sem["sum%d_%d" % (ci, gi)], PLAN["arrive"][core][(ci, gi)])
+        q.dma_start(T.s_sb[ci * H + row // NPL:ci * H + (row + w * cnt) // NPL, :],
+                    T["sum%d_%d" % (ci, gi)][:]).then_inc(T.sem["in%d_%d" % (ci, gi)], 16)
 
-    ops = [(T.x_sb, None)] * extra
-    for ci in order:
-        ops += [(T["s%d_sb" % ci], T.sem["in%d" % ci])] + [(T["s%d_sb" % ci], None)] * (u - 1)
-    g.tensor.wait_ge(T.sem.ld, 32)
-    for i, (rhs, sem) in enumerate(ops):
-        if sem is not None:
-            g.tensor.wait_ge(sem, 16)
-        mm = g.tensor.matmul(T.acc[:], T.a_sb[:], rhs[:], i == 0, i == len(ops) - 1)
+    ops = []
+    for _ in range(extra):
+        for t in range(NPL):
+            ops.append((T.a_sb[0:H, t * W:(t + 1) * W], T.x_sb[:, t * W:(t + 1) * W], False))
+    for n in range(u):
+        for t in range(NPL):
+            ops.append((T.a_sb[:, t * W:(t + 1) * W], T.s_sb[:, t * W:(t + 1) * W], n == 0 and t == 0))
+    g.tensor.wait_ge(T.sem.ld, 16 * (NPL + 1))
+    for i, (lhsT, rhs, first) in enumerate(ops):
+        if first:
+            for (gi, ci) in loads:
+                g.tensor.wait_ge(T.sem["in%d_%d" % (ci, gi)], 16)
+        mm = g.tensor.matmul(T.acc[:], lhsT, rhs, i == 0, i == len(ops) - 1)
     mm.then_inc(T.sem.mm, 1)
     g.vector.wait_ge(T.sem.mm, 1)
     g.vector.tensor_copy(T.y_sb[:], T.acc[:]).then_inc(T.sem.cp, 1)

import comms_topo
from concourse.bass import DstId, RemoteDMATransfer

CORES = [3, 5, 43, 45, 51, 53, 67, 69, 75, 77, 83, 85, 91, 93, 115, 117]
P, W = 128, 128


def _engines(mask):
    return [e for e in range(mask.bit_length()) if (mask >> e) & 1]


def _mask_of(engines):
    m = 0
    for e in engines:
        m |= 1 << e
    return m


def _pow2_floor(n):
    k = 1
    while 2 * k <= n:
        k *= 2
    return k


def _turn(lst, s, k):
    o = (s * len(lst)) // k
    return lst[o:] + lst[:o]


def _make_plan(cores, topo):
    planes = []
    for c in cores:
        for pl in planes:
            if topo.chip(pl[0]) == topo.chip(c) or topo.same_plane(topo.chip(pl[0]), topo.chip(c)):
                pl.append(c)
                break
        else:
            planes.append([c])
    npl = len(planes)

    def cut(k):
        w = -(-P // k)
        w += (-w) % npl
        return [w] * (k - 1) + [P - w * (k - 1)]

    who = []
    for mem in planes:
        far = [c for c in cores if c not in mem]
        ported = [m for m in mem if all(topo.may_write(m, d) for d in far)]
        who.append((far, ported, [m for m in mem if m not in ported]))

    def work(ci, k):
        return (len(planes[ci]) + max(len(who[ci][0]) + 1, len(cores) // 2)) * cut(k)[0]

    kmax = [min(len(p), len(i)) for (_, p, i) in who]
    bound = max(min(work(ci, kmax[ci]), work(ci, _pow2_floor(kmax[ci]))) for ci in range(npl))
    widths, jobs = [], []
    for ci, mem in enumerate(planes):
        far, ported, inner = who[ci]
        k = _pow2_floor(kmax[ci]) if work(ci, _pow2_floor(kmax[ci])) <= bound else kmax[ci]
        widths.append(cut(k))
        load = {}
        for m in ported[:k]:
            load[topo.chip(m)] = load.get(topo.chip(m), 0) + 1
        own_in = []
        for s in range(k):
            b = min([m for m in inner if m not in own_in], key=lambda m: load.get(topo.chip(m), 0))
            load[topo.chip(b)] = load.get(topo.chip(b), 0) + 1
            own_in.append(b)
        for s in range(k):
            p, b = ported[s], own_in[s]
            free = sorted([m for m in mem if m not in (p, b)], key=lambda m: topo.chip(m) != topo.chip(p))
            take = free[:max(0, (len(free) - len(far)) // 2)]
            jobs.append([ci, b, s, _turn([m for m in mem if m != b and m not in take], s, k)])
            jobs.append([ci, p, s, _turn(list(far), s, k) + take + [b]])
    groups, place = [], []
    for ci in range(npl):
        gr, pl, row = [], [], 0
        for w in widths[ci]:
            if not gr or gr[-1][1] != w:
                gr.append([row, w, 0])
            pl.append((len(gr) - 1, gr[-1][2]))
            gr[-1][2] += 1
            row += w
        groups.append(gr)
        place.append(pl)
    send = {}
    for ci, mem in enumerate(planes):
        for m in mem:
            eng = _engines(topo.mask(m, who[ci][0][0]))
            calls = []
            for gi in range(len(groups[ci])):
                trs = []
                for s in range(len(widths[ci])):
                    if place[ci][s][0] != gi:
                        continue
                    ds = [o for (cj, o, s2, _) in jobs if cj == ci and s2 == s and o != m]
                    ds.sort(key=lambda o: topo.chip(o) == topo.chip(m))
                    assert all(topo.mask(m, o) & _mask_of(eng) == _mask_of(eng) for o in ds)
                    trs.append((ds, s))
                per = _pow2_floor(len(eng) // len(trs))
                calls.append([(ds, s, eng[i * per:(i + 1) * per]) for i, (ds, s) in enumerate(trs)])
            send[m] = calls
    serve = {}
    for (ci, c, s, dests) in jobs:
        assert c not in serve
        common = None
        for d in dests:
            common = topo.mask(c, d) if common is None else common & topo.mask(c, d)
        serve[c] = (ci, s, dests, _engines(common))
    got = {c: 0 for c in cores}
    for m in send:
        for call in send[m]:
            for (ds, s, e) in call:
                for o in ds:
                    got[o] += len(e)
    arrive = {c: {} for c in cores}
    cover = {c: [] for c in cores}
    for c in serve:
        ci, s, dests, e = serve[c]
        for d in dests:
            assert d != c and topo.may_write(c, d)
            key = (ci, place[ci][s][0])
            arrive[d][key] = arrive[d].get(key, 0) + len(e)
            cover[d].append((ci, s))
    want = sorted((ci, s) for ci in range(npl) for s in range(len(widths[ci])))
    for c in cores:
        assert sorted(cover[c]) == want
    return {"planes": planes, "groups": groups, "place": place, "send": send, "serve": serve, "got": got,
            "arrive": arrive}


PLAN = _make_plan(CORES, comms_topo)
NPL = len(PLAN["planes"])
H = P // NPL
assert H * NPL == P and H % 32 == 0

SCRATCH = {
    "a_sb": ("sbuf", [P, NPL * W], "bfloat16"),
    "x_sb": ("sbuf", [H, NPL * W], "bfloat16"),
    "s_sb": ("sbuf", [P, NPL * W], "bfloat16"),
    "y_sb": ("sbuf", [P, W], "bfloat16"),
    "acc": ("psum", [P, W], "float32"),
}
SEMAPHORES = ["ld", "got", "sent", "mm", "cp", "st"]
for _ci, _gr in enumerate(PLAN["groups"]):
    _n = len(PLAN["planes"][_ci])
    for _gi, (_row, _w, _cnt) in enumerate(_gr):
        SCRATCH["xd%d_%d" % (_ci, _gi)] = ("dram", [_cnt, P, _w], "bfloat16")
        SCRATCH["land%d_%d" % (_ci, _gi)] = ("dram", [_n, P, _w], "bfloat16")
        SCRATCH["sum%d_%d" % (_ci, _gi)] = ("dram", [_cnt, P, _w], "bfloat16")
        SEMAPHORES += ["sum%d_%d" % (_ci, _gi), "in%d_%d" % (_ci, _gi)]
for _gi in range(max(len(_gr) for _gr in PLAN["groups"])):
    SEMAPHORES.append("xd%d" % _gi)


def rank_program(g, core, T, topo):
    rank = T.rank_of(core)
    if rank is None:
        return
    assert list(T.cores) == CORES
    coef = T.tables["COEF"]
    u = coef[0][1]
    assert all(coef[r][j] == u for r in range(len(CORES)) for j in range(len(CORES)) if r != j) and u >= 1
    extra = coef[rank][rank] - u
    assert extra >= 0

    planes, groups, place = PLAN["planes"], PLAN["groups"], PLAN["place"]
    mine = [ci for ci, mem in enumerate(planes) if core in mem][0]
    mem = planes[mine]
    queues = [g.sync, g.scalar]

    def dst_id(c):
        rid, pid, _ = topo.addr(c)
        return DstId(rid=rid, pnc=pid)

    def xd(s):
        gi, i = place[mine][s]
        return T["xd%d_%d" % (mine, gi)][i]

    for gi, (row, w, cnt) in enumerate(groups[mine]):
        queues[gi % 2].dma_start(T["xd%d_%d" % (mine, gi)][:], T.x[row:row + w * cnt, :]).then_inc(T.sem["xd%d" % gi], 16)
    for ci in range(NPL):
        g.sync.dma_start(T.a_sb[ci * H:(ci + 1) * H, :], T.a[:]).then_inc(T.sem.ld, 16)
    g.sync.dma_start(T.x_sb[:], T.x[:]).then_inc(T.sem.ld, 16)

    sent = 0
    for gi, call in enumerate(PLAN["send"][core]):
        g.wait_ge(T.sem["xd%d" % gi], 16)
        out = []
        for (ds, s, eng) in call:
            out.append(RemoteDMATransfer(dst_ids=[dst_id(o) for o in ds], dma_engine_mask=_mask_of(eng),
                                         remote_sem=T.sem.got, srcs=[xd(s)],
                                         dsts=[T["land%d_%d" % (mine, gi)][mem.index(core)] for _ in ds], alu_op=0))
            sent += len(eng)
        g.remote_dma_fused(out, local_sem=T.sem.sent)

    if core in PLAN["serve"]:
        ci, s, dests, eng = PLAN["serve"][core]
        gi, i = place[ci][s]
        g.wait_ge(T.sem.got, PLAN["got"][core])
        srcs = [xd(s) if m == core else T["land%d_%d" % (ci, gi)][j] for j, m in enumerate(mem)]
        g.remote_dma_fused([RemoteDMATransfer(dst_ids=[dst_id(d) for d in dests], dma_engine_mask=_mask_of(eng),
                                              remote_sem=T.sem["sum%d_%d" % (ci, gi)], srcs=srcs,
                                              dsts=[T["sum%d_%d" % (ci, gi)][i] for _ in dests], alu_op=1)],
                           local_sem=T.sem.sent)
        sent += len(eng)
    g.wait_ge(T.sem.sent, sent)

    loads = sorted((gi, ci) for ci in range(NPL) for gi in range(len(groups[ci])))
    for i, (gi, ci) in enumerate(loads):
        row, w, cnt = groups[ci][gi]
        q = queues[i % 2]
        q.wait_ge(T.sem["sum%d_%d" % (ci, gi)], PLAN["arrive"][core][(ci, gi)])
        q.dma_start(T.s_sb[ci * H + row // NPL:ci * H + (row + w * cnt) // NPL, :],
                    T["sum%d_%d" % (ci, gi)][:]).then_inc(T.sem["in%d_%d" % (ci, gi)], 16)

    ops = []
    for _ in range(extra):
        for t in range(NPL):
            ops.append((T.a_sb[0:H, t * W:(t + 1) * W], T.x_sb[:, t * W:(t + 1) * W], False))
    for n in range(u):
        for t in range(NPL):
            ops.append((T.a_sb[:, t * W:(t + 1) * W], T.s_sb[:, t * W:(t + 1) * W], n == 0 and t == 0))
    g.tensor.wait_ge(T.sem.ld, 16 * (NPL + 1))
    for i, (lhsT, rhs, first) in enumerate(ops):
        if first:
            for (gi, ci) in loads:
                g.tensor.wait_ge(T.sem["in%d_%d" % (ci, gi)], 16)
        mm = g.tensor.matmul(T.acc[:], lhsT, rhs, i == 0, i == len(ops) - 1)
    mm.then_inc(T.sem.mm, 1)
    g.vector.wait_ge(T.sem.mm, 1)
    g.vector.tensor_copy(T.y_sb[:], T.acc[:]).then_inc(T.sem.cp, 1)
    g.sync.wait_ge(T.sem.cp, 1)
    g.sync.dma_start(T.y[:], T.y_sb[:]).then_inc(T.sem.st, 16)
    g.sync.wait_ge(T.sem.st, 16)
